import numpy as np
import ml_dtypes


def mxq(x, axis, fmt="e4m3"):
    dtype, down = {"e4m3": (ml_dtypes.float8_e4m3fn, 7), "e5m2": (ml_dtypes.float8_e5m2, 14)}[fmt]
    v = np.moveaxis(np.asarray(x, np.float32).astype(ml_dtypes.bfloat16).astype(np.float64), axis, -1)
    blocks = v.reshape(v.shape[:-1] + (-1, 32))
    amax = np.abs(blocks).max(-1, keepdims=True)
    byte = np.maximum(np.where(amax > 0, np.frexp(amax)[1] - 1 + 127, 0) - down, 1)
    scale = np.exp2(byte - 127.0)
    codes = (blocks / scale).astype(np.float32).astype(dtype).astype(np.float64)
    return np.moveaxis((codes * scale).reshape(v.shape), -1, axis)


WIDE = False


def mx_kscale(k):
    if not WIDE:
        return np.ones(k)
    levels = np.array([10, -10, 5, -5, 0])
    if k % 512:
        return np.exp2(np.random.permutation(np.resize(levels, k // 32))).repeat(32)
    a = np.empty((k // 512, 16))
    for p in range(k // 512):
        a[p, :8] = np.random.permutation(np.resize(levels, 8))
        for g in range(8):
            far = levels[np.abs(levels - a[p, g]) >= 10]
            a[p, g + 8] = far[np.random.randint(len(far))]
    return np.exp2(a.ravel()).repeat(32)


def f64(x):
    return np.asarray(x).astype(np.float64)


def striped(idx):
    return np.tile(idx.reshape(-1, 16).T, (8, 1)).astype(np.uint16)


def unstriped(offs):
    return offs[:16].T.reshape(-1).astype(np.int64)


def pack_weight(w):
    k, n = w.shape
    w = f64(np.asarray(w, np.float32).astype(ml_dtypes.bfloat16)).reshape(k // 32, 32, n)
    amax = np.abs(w).max(1)
    byte = np.clip(np.where(amax > 0, np.frexp(amax)[1] - 1 + 127 - 7, 1), 1, 254)
    scaled = (w * np.exp2(127.0 - byte)[:, None, :]).reshape(k, n).astype(np.float32)
    words = np.ascontiguousarray(scaled.reshape(k // 512, 128, 4, n).transpose(0, 1, 3, 2)).astype(ml_dtypes.float8_e4m3fn).view(np.uint8)
    return words, np.ascontiguousarray(byte.astype(np.uint8).reshape(k // 512, 16, n))


def unpack_weight(words, scales):
    g, p, n, _ = words.shape
    vals = np.ascontiguousarray(words).view(ml_dtypes.float8_e4m3fn).astype(np.float64) * np.repeat(np.exp2(scales.astype(np.float64) - 127.0), 8, axis=1)[..., None]
    return vals.transpose(0, 1, 3, 2).reshape(g * 512, n)


def sigmoid(v):
    return 1.0 / (1.0 + np.exp(-np.maximum(v, -700.0)))


K, T, S, D, N = 512, 2048, 512, 2, 256
P = 2 ** 7


def setup_inputs():
    n = np.random.standard_normal
    s = mx_kscale(K)[:, None]
    packed_xT = pack_weight(n((K, T)) * s)
    return {
        "x_words": packed_xT[0],
        "x_scales": packed_xT[1],
        "w1": (n((K, N)) / np.sqrt(K) / s).astype(np.float32),
        "w2": (n((K, N)) / np.sqrt(K) / s).astype(np.float32),
        "depth": (np.tile(np.random.uniform(0.2, 2.0, S), (P, 1))).astype(np.float32),
        "offs": striped(np.random.permutation(T)[:S]),
    }


def reference(x_words, x_scales, w1, w2, depth, offs):
    xq = unpack_weight(x_words, x_scales)[:, unstriped(offs)]
    a = 0.95 * (sigmoid(mxq(f64(w2), 0, "e4m3").T @ xq))
    ww = a * f64(depth)[:1]
    col = mxq(f64(w1), 0, "e4m3").T @ xq
    cw = ww * col
    den = ww.reshape(len(ww), -1, D).sum(axis=2) + 0.05
    avg = (cw.reshape(len(cw), -1, D).sum(axis=2)) / den
    lt = np.log(-1.0 * a + 1.0)
    tr = np.exp(lt.reshape(len(lt), -1, D).sum(axis=2))
    return avg - (avg * tr) + 0.5 * tr

@@ -1,0 +1,172 @@
+from contextlib import ExitStack
+
+import concourse.mybir as mybir
+from concourse.masks import make_identity
+
+K, T, S, D, N = 512, 2048, 512, 2, 256
+FLOPS = 2 * 2 * K * N * S
+
+F32 = mybir.dt.float32
+BF16 = mybir.dt.bfloat16
+I32 = mybir.dt.int32
+U32 = mybir.dt.uint32
+U16 = mybir.dt.uint16
+U8 = mybir.dt.uint8
+FP8X4 = mybir.dt.float8_e4m3fn_x4
+ALU = mybir.AluOpType
+ACT = mybir.ActivationFunctionType
+
+P = 128
+PACK = 4
+BLOCKS = S // (D * P)
+MB = N // P
+OPACITY = 0.95
+EPS = 0.05
+GREY = 0.5
+
+
+def interleave(copy, grouped, raw):
+    copy(
+        grouped[:].rearrange("p (c i) t -> p c t i", i=4),
+        raw[:].rearrange("p t (c i) -> p c t i", i=4),
+    )
+
+
+def tile_picked_yoit_grey_p_kernel(tc, x_words, x_scales, w1, w2, depth, offs, out):
+    nc = tc.nc
+    with ExitStack() as ctx:
+        sb = ctx.enter_context(tc.tile_pool(name="sb", bufs=1))
+        ps = ctx.enter_context(tc.psum_pool(name="ps", bufs=1))
+
+        offsets = sb.tile([P, S // 16], U16, name="offsets")
+        nc.sync.dma_start(offsets[:], offs)
+
+        scale_table = sb.tile([P, T], U8, name="scale_table", align_bytes=64)
+        nc.vector.memset(scale_table[:].bitcast(I32), 0)
+        warm_in = sb.tile([P, 1], F32, name="warm_in")
+        nc.vector.memset(warm_in[:], 0.0)
+
+        w2_raw = sb.tile([P, PACK, N], F32, name="w2_raw")
+        nc.sync.dma_start(w2_raw[:], w2.rearrange("(p j) n -> p j n", j=PACK))
+        word_table = sb.tile([P, T], U32, name="word_table", align_bytes=64)
+        nc.sync.dma_start(word_table[:].bitcast(I32), x_words[0].rearrange("p n t -> p (n t)").bitcast(I32))
+        w1_raw = sb.tile([P, PACK, N], F32, name="w1_raw")
+        nc.sync.dma_start(w1_raw[:], w1.rearrange("(p j) n -> p j n", j=PACK))
+
+        for q in range(4):
+            nc.scalar.dma_start(
+                scale_table[32 * q : 32 * q + 4, :].bitcast(I32), x_scales[0, 4 * q : 4 * q + 4, :].bitcast(I32)
+            )
+        dep = sb.tile([P, BLOCKS, D], F32, name="dep")
+        nc.scalar.dma_start(dep[:], depth[0].rearrange("(b p d) -> p b d", p=P, d=D))
+
+        warm_out = sb.tile([P, 1], F32, name="warm_out")
+        nc.scalar.activation(warm_out[:], warm_in[:], ACT.Sigmoid)
+
+        ident = sb.tile([P, P], F32, name="ident")
+        make_identity(nc, ident[:])
+
+        w2_bf = sb.tile([P, N, PACK], BF16, name="w2_bf", align_bytes=64)
+        interleave(nc.scalar.copy, w2_bf, w2_raw)
+
+        picked_scales = sb.tile([P, S], U8, name="picked_scales", align_bytes=64)
+        nc.vector.tensor_copy(picked_scales[:], scale_table[:].indirect(offsets[:]))
+        x_sc = sb.tile([P, BLOCKS, D, P], U8, name="x_sc", align_bytes=64)
+        nc.vector.tensor_copy(x_sc[:], picked_scales[:].rearrange("p (b v d) -> p b d v", b=BLOCKS, d=D))
+
+        w2_codes = sb.tile([P, N], U32, name="w2_codes", align_bytes=64)
+        w2_sc = sb.tile([P, N], U8, name="w2_sc", align_bytes=64)
+        nc.vector.quantize_mx(w2_codes[:].bitcast(FP8X4), w2_sc[:], w2_bf[:].rearrange("p n t -> p (n t)"))
+
+        cols = S // 16 // BLOCKS
+        x_codes = []
+        for b in range(BLOCKS):
+            t = sb.tile([P, D, P], U32, name=f"x_codes{b}", align_bytes=64)
+            nc.vector.tensor_copy(
+                t[:].rearrange("p d v -> p v d"), word_table[:].indirect(offsets[:, b * cols : (b + 1) * cols])
+            )
+            x_codes.append(t)
+
+        def product(bank, b, codes, sc):
+            for d in range(D):
+                nc.tensor.matmul_mx(
+                    bank[:, d, :],
+                    lhsT=x_codes[b][:, d, :].bitcast(FP8X4),
+                    lhsT_scale=x_sc[:, b, d, :],
+                    rhs=codes[:].bitcast(FP8X4),
+                    rhs_scale=sc[:],
+                    start=True,
+                    stop=True,
+                )
+
+        sig = []
+        for b in range(BLOCKS):
+            logit = ps.tile([P, D, N], F32, name=f"logit{b}")
+            product(logit, b, w2_codes, w2_sc)
+            s = sb.tile([P, D, N], F32, name=f"sig{b}")
+            nc.scalar.activation(s[:], logit[:], ACT.Sigmoid)
+            sig.append(s)
+
+        w1_bf = sb.tile([P, N, PACK], BF16, name="w1_bf", align_bytes=64)
+        interleave(nc.vector.tensor_copy, w1_bf, w1_raw)
+        w1_codes = sb.tile([P, N], U32, name="w1_codes", align_bytes=64)
+        w1_sc = sb.tile([P, N], U8, name="w1_sc", align_bytes=64)
+        nc.vector.quantize_mx(w1_codes[:].bitcast(FP8X4), w1_sc[:], w1_bf[:].rearrange("p n t -> p (n t)"))
+
+        colour = []
+        for b in range(BLOCKS):
+            c = ps.tile([P, D, N], F32, name=f"colour{b}")
+            product(c, b, w1_codes, w1_sc)
+            colour.append(c)
+
+        def turn(dst, parts):
+            for m in range(MB):
+                for i, part in enumerate(parts):
+                    nc.tensor.matmul(
+                        dst[:, m, :],
+                        lhsT=part[:, m * P : (m + 1) * P],
+                        rhs=ident[:],
+                        start=(i == 0),
+                        stop=(i == len(parts) - 1),
+                        is_transpose=True,
+                    )
+
+        ww, den = [], []
+        for b in range(BLOCKS):
+            w = sb.tile([P, D, N], F32, name=f"ww{b}")
+            for d in range(D):
+                nc.vector.tensor_scalar(w[:, d, :], sig[b][:, d, :], dep[:, b, d : d + 1], OPACITY, ALU.mult, ALU.mult)
+            ww.append(w)
+            dn = ps.tile([P, MB, P], F32, name=f"den{b}")
+            turn(dn, [w[:, 0, :], w[:, 1, :]])
+            den.append(dn)
+
+        turned = []
+        for b in range(BLOCKS):
+            cw = sb.tile([P, D, N], F32, name=f"cw{b}")
+            nc.vector.scalar_tensor_tensor(cw[:], colour[b][:], GREY, ww[b][:], ALU.subtract, ALU.mult)
+            q = sb.tile([P, N], F32, name=f"q{b}")
+            nc.vector.tensor_scalar(q[:], sig[b][:, 1, :], 1.0 / OPACITY, None, ALU.subtract)
+            tr = sb.tile([P, N], F32, name=f"tr{b}")
+            nc.vector.scalar_tensor_tensor(tr[:], sig[b][:, 0, :], 1.0 / OPACITY, q[:], ALU.subtract, ALU.mult)
+            both = ps.tile([P, 2, MB, P], F32, name=f"turned{b}")
+            turn(both[:, 0], [cw[:, 0, :], cw[:, 1, :]])
+            turn(both[:, 1], [tr[:]])
+            turned.append(both)
+
+        for b in range(BLOCKS):
+            rs = sb.tile([P, MB, P], F32, name=f"rs{b}")
+            nc.scalar.activation(rs[:], den[b][:], ACT.Abs_reciprocal_sqrt, bias=EPS)
+            r = sb.tile([P, MB, P], F32, name=f"r{b}")
+            nc.scalar.activation(r[:], rs[:], ACT.Square)
+            sg = sb.tile([P, MB, P], F32, name=f"sg{b}")
+            nc.scalar.activation(sg[:], den[b][:], ACT.Sign, bias=EPS)
+            g = sb.tile([P, MB, P], F32, name=f"g{b}")
+            nc.vector.scalar_tensor_tensor(g[:], turned[b][:, 1], 1.0 / OPACITY**2, sg[:], ALU.subtract, ALU.mult)
+            avg = sb.tile([P, MB, P], F32, name=f"avg{b}")
+            nc.vector.scalar_tensor_tensor(avg[:], turned[b][:, 0], EPS * GREY, r[:], ALU.subtract, ALU.mult)
+            h = sb.tile([P, MB, P], F32, name=f"h{b}")
+            nc.vector.tensor_tensor(h[:], avg[:], g[:], ALU.mult)
+            res = sb.tile([P, MB, P], F32, name=f"res{b}")
+            nc.scalar.activation(res[:], h[:], ACT.Copy, bias=GREY, scale=-(OPACITY**2))
+            nc.sync.dma_start(out[:, b * P : (b + 1) * P].rearrange("(m p) v -> p m v", p=P), res[:])

@@ -23,12 +23,13 @@ MB = N // P
 OPACITY = 0.95
 EPS = 0.05
 GREY = 0.5
+SCALAR_SHARE = 96
 
 
-def interleave(copy, grouped, raw):
+def interleave(copy, grouped, raw, cols):
     copy(
-        grouped[:].rearrange("p (c i) t -> p c t i", i=4),
-        raw[:].rearrange("p t (c i) -> p c t i", i=4),
+        grouped[:, cols, :].rearrange("p (c i) t -> p c t i", i=4),
+        raw[:, :, cols].rearrange("p t (c i) -> p c t i", i=4),
     )
 
 
@@ -38,27 +39,25 @@ def tile_picked_yoit_grey_p_kernel(tc, x_words, x_scales, w1, w2, depth, offs, o
         sb = ctx.enter_context(tc.tile_pool(name="sb", bufs=1))
         ps = ctx.enter_context(tc.psum_pool(name="ps", bufs=1))
 
-        offsets = sb.tile([P, S // 16], U16, name="offsets")
-        nc.sync.dma_start(offsets[:], offs)
-
         scale_table = sb.tile([P, T], U8, name="scale_table", align_bytes=64)
-        nc.vector.memset(scale_table[:].bitcast(I32), 0)
+        nc.gpsimd.memset(scale_table[:].bitcast(I32), 0)
         warm_in = sb.tile([P, 1], F32, name="warm_in")
         nc.vector.memset(warm_in[:], 0.0)
 
         w2_raw = sb.tile([P, PACK, N], F32, name="w2_raw")
         nc.sync.dma_start(w2_raw[:], w2.rearrange("(p j) n -> p j n", j=PACK))
-        word_table = sb.tile([P, T], U32, name="word_table", align_bytes=64)
-        nc.sync.dma_start(word_table[:].bitcast(I32), x_words[0].rearrange("p n t -> p (n t)").bitcast(I32))
-        w1_raw = sb.tile([P, PACK, N], F32, name="w1_raw")
-        nc.sync.dma_start(w1_raw[:], w1.rearrange("(p j) n -> p j n", j=PACK))
-
+        offsets = sb.tile([P, S // 16], U16, name="offsets")
+        nc.sync.dma_start(offsets[:], offs)
         for q in range(4):
-            nc.scalar.dma_start(
+            nc.sync.dma_start(
                 scale_table[32 * q : 32 * q + 4, :].bitcast(I32), x_scales[0, 4 * q : 4 * q + 4, :].bitcast(I32)
             )
+        word_table = sb.tile([P, T], U32, name="word_table", align_bytes=64)
+        nc.sync.dma_start(word_table[:].bitcast(I32), x_words[0].rearrange("p n t -> p (n t)").bitcast(I32))
+        w1_raw = sb.tile([P, PACK, N], F32, name="w1_raw", tag="sig")
+        nc.sync.dma_start(w1_raw[:], w1.rearrange("(p j) n -> p j n", j=PACK))
         dep = sb.tile([P, BLOCKS, D], F32, name="dep")
-        nc.scalar.dma_start(dep[:], depth[0].rearrange("(b p d) -> p b d", p=P, d=D))
+        nc.sync.dma_start(dep[:], depth[0].rearrange("(b p d) -> p b d", p=P, d=D))
 
         warm_out = sb.tile([P, 1], F32, name="warm_out")
         nc.scalar.activation(warm_out[:], warm_in[:], ACT.Sigmoid)
@@ -67,15 +66,15 @@ def tile_picked_yoit_grey_p_kernel(tc, x_words, x_scales, w1, w2, depth, offs, o
         make_identity(nc, ident[:])
 
         w2_bf = sb.tile([P, N, PACK], BF16, name="w2_bf", align_bytes=64)
-        interleave(nc.scalar.copy, w2_bf, w2_raw)
+        interleave(nc.scalar.copy, w2_bf, w2_raw, slice(0, N))
 
-        picked_scales = sb.tile([P, S], U8, name="picked_scales", align_bytes=64)
+        picked_scales = sb.tile([P, S], U8, name="picked_scales", tag="picked_scales", align_bytes=64)
         nc.vector.tensor_copy(picked_scales[:], scale_table[:].indirect(offsets[:]))
         x_sc = sb.tile([P, BLOCKS, D, P], U8, name="x_sc", align_bytes=64)
         nc.vector.tensor_copy(x_sc[:], picked_scales[:].rearrange("p (b v d) -> p b d v", b=BLOCKS, d=D))
 
         w2_codes = sb.tile([P, N], U32, name="w2_codes", align_bytes=64)
-        w2_sc = sb.tile([P, N], U8, name="w2_sc", align_bytes=64)
+        w2_sc = sb.tile([P, N], U8, name="w2_sc", tag="picked_scales", align_bytes=64)
         nc.vector.quantize_mx(w2_codes[:].bitcast(FP8X4), w2_sc[:], w2_bf[:].rearrange("p n t -> p (n t)"))
 
         cols = S // 16 // BLOCKS
@@ -99,16 +98,20 @@ def tile_picked_yoit_grey_p_kernel(tc, x_words, x_scales, w1, w2, depth, offs, o
                     stop=True,
                 )
 
-        sig = []
-        for b in range(BLOCKS):
-            logit = ps.tile([P, D, N], F32, name=f"logit{b}")
-            product(logit, b, w2_codes, w2_sc)
-            s = sb.tile([P, D, N], F32, name=f"sig{b}")
-            nc.scalar.activation(s[:], logit[:], ACT.Sigmoid)
-            sig.append(s)
+        w1_bf = sb.tile([P, N, PACK], BF16, name="w1_bf", tag="ww", align_bytes=64)
+        interleave(nc.scalar.copy, w1_bf, w1_raw, slice(0, SCALAR_SHARE))
+        interleave(nc.vector.tensor_copy, w1_bf, w1_raw, slice(SCALAR_SHARE, N))
 
-        w1_bf = sb.tile([P, N, PACK], BF16, name="w1_bf", align_bytes=64)
-        interleave(nc.vector.tensor_copy, w1_bf, w1_raw)
+        sig_all = sb.tile([P, BLOCKS, D, N], F32, name="sig_all", tag="sig")
+        sig = [sig_all[:, b] for b in range(BLOCKS)]
+        for b in range(BLOCKS):
+            logit = ps.tile([P, D, N], F32, name=f"logit{b}", tag=f"logit{b}")
+            product(logit, b, w2_codes, w2_sc)
+            nc.scalar.activation(sig[b], logit[:], ACT.Sigmoid)
+
+        warm2 = sb.tile([P, BLOCKS], F32, name="warm2")
+        nc.scalar.activation(warm2[:], sig_all[:, :, 0, 0], ACT.Abs_reciprocal_sqrt, bias=1.0)
+
         w1_codes = sb.tile([P, N], U32, name="w1_codes", align_bytes=64)
         w1_sc = sb.tile([P, N], U8, name="w1_sc", align_bytes=64)
         nc.vector.quantize_mx(w1_codes[:].bitcast(FP8X4), w1_sc[:], w1_bf[:].rearrange("p n t -> p (n t)"))
@@ -131,42 +134,52 @@ def tile_picked_yoit_grey_p_kernel(tc, x_words, x_scales, w1, w2, depth, offs, o
                         is_transpose=True,
                     )
 
-        ww, den = [], []
+        ww_all = sb.tile([P, BLOCKS, D, N], F32, name="ww_all", tag="ww", align_bytes=64)
+        ww, den, shifted = [], [], []
         for b in range(BLOCKS):
-            w = sb.tile([P, D, N], F32, name=f"ww{b}")
+            w = ww_all[:, b]
             for d in range(D):
                 nc.vector.tensor_scalar(w[:, d, :], sig[b][:, d, :], dep[:, b, d : d + 1], OPACITY, ALU.mult, ALU.mult)
             ww.append(w)
+            q = sb.tile([P, N], F32, name=f"q{b}")
+            nc.vector.tensor_scalar(q[:], sig[b][:, 1, :], 1.0 / OPACITY, None, ALU.subtract)
+            shifted.append(q)
             dn = ps.tile([P, MB, P], F32, name=f"den{b}")
             turn(dn, [w[:, 0, :], w[:, 1, :]])
             den.append(dn)
 
-        turned = []
+        through = []
+        for b in range(BLOCKS):
+            tr = sb.tile([P, N], F32, name=f"tr{b}")
+            nc.vector.scalar_tensor_tensor(tr[:], sig[b][:, 0, :], 1.0 / OPACITY, shifted[b][:], ALU.subtract, ALU.mult)
+            th = ps.tile([P, MB, P], F32, name=f"through{b}")
+            turn(th, [tr[:]])
+            through.append(th)
+
+        num = []
         for b in range(BLOCKS):
             cw = sb.tile([P, D, N], F32, name=f"cw{b}")
-            nc.vector.scalar_tensor_tensor(cw[:], colour[b][:], GREY, ww[b][:], ALU.subtract, ALU.mult)
-            q = sb.tile([P, N], F32, name=f"q{b}")
-            nc.vector.tensor_scalar(q[:], sig[b][:, 1, :], 1.0 / OPACITY, None, ALU.subtract)
-            tr = sb.tile([P, N], F32, name=f"tr{b}")
-            nc.vector.scalar_tensor_tensor(tr[:], sig[b][:, 0, :], 1.0 / OPACITY, q[:], ALU.subtract, ALU.mult)
-            both = ps.tile([P, 2, MB, P], F32, name=f"turned{b}")
-            turn(both[:, 0], [cw[:, 0, :], cw[:, 1, :]])
-            turn(both[:, 1], [tr[:]])
-            turned.append(both)
+            nc.vector.scalar_tensor_tensor(cw[:], colour[b][:], GREY, ww[b], ALU.subtract, ALU.mult)
+            nm = ps.tile([P, MB, P], F32, name=f"num{b}", tag=f"logit{b}")
+            turn(nm, [cw[:, 0, :], cw[:, 1, :]])
+            num.append(nm)
 
         for b in range(BLOCKS):
+            sg = sb.tile([P, MB, P], F32, name=f"sg{b}")
             rs = sb.tile([P, MB, P], F32, name=f"rs{b}")
             nc.scalar.activation(rs[:], den[b][:], ACT.Abs_reciprocal_sqrt, bias=EPS)
+            nc.scalar.activation(sg[:], den[b][:], ACT.Sign, bias=EPS)
             r = sb.tile([P, MB, P], F32, name=f"r{b}")
             nc.scalar.activation(r[:], rs[:], ACT.Square)
-            sg = sb.tile([P, MB, P], F32, name=f"sg{b}")
-            nc.scalar.activation(sg[:], den[b][:], ACT.Sign, bias=EPS)
             g = sb.tile([P, MB, P], F32, name=f"g{b}")
-            nc.vector.scalar_tensor_tensor(g[:], turned[b][:, 1], 1.0 / OPACITY**2, sg[:], ALU.subtract, ALU.mult)
-            avg = sb.tile([P, MB, P], F32, name=f"avg{b}")
-            nc.vector.scalar_tensor_tensor(avg[:], turned[b][:, 0], EPS * GREY, r[:], ALU.subtract, ALU.mult)
+            nc.vector.scalar_tensor_tensor(g[:], through[b][:], 1.0 / OPACITY**2, sg[:], ALU.subtract, ALU.mult)
+            gr = sb.tile([P, MB, P], F32, name=f"gr{b}")
+            nc.vector.scalar_tensor_tensor(gr[:], g[:], -(OPACITY**2), r[:], ALU.mult, ALU.mult)
             h = sb.tile([P, MB, P], F32, name=f"h{b}")
-            nc.vector.tensor_tensor(h[:], avg[:], g[:], ALU.mult)
+            nc.vector.scalar_tensor_tensor(h[:], num[b][:], EPS * GREY, gr[:], ALU.subtract, ALU.mult)
             res = sb.tile([P, MB, P], F32, name=f"res{b}")
-            nc.scalar.activation(res[:], h[:], ACT.Copy, bias=GREY, scale=-(OPACITY**2))
+            if b < BLOCKS - 1:
+                nc.scalar.activation(res[:], h[:], ACT.Copy, bias=GREY)
+            else:
+                nc.vector.tensor_scalar(res[:], h[:], GREY, None, ALU.add)
             nc.sync.dma_start(out[:, b * P : (b + 1) * P].rearrange("(m p) v -> p m v", p=P), res[:])

@@ -23,7 +23,7 @@ MB = N // P
 OPACITY = 0.95
 EPS = 0.05
 GREY = 0.5
-SCALAR_SHARE = 96
+SCALAR_SHARE = 128
 
 
 def interleave(copy, grouped, raw, cols):
@@ -86,17 +86,16 @@ def tile_picked_yoit_grey_p_kernel(tc, x_words, x_scales, w1, w2, depth, offs, o
             )
             x_codes.append(t)
 
-        def product(bank, b, codes, sc):
-            for d in range(D):
-                nc.tensor.matmul_mx(
-                    bank[:, d, :],
-                    lhsT=x_codes[b][:, d, :].bitcast(FP8X4),
-                    lhsT_scale=x_sc[:, b, d, :],
-                    rhs=codes[:].bitcast(FP8X4),
-                    rhs_scale=sc[:],
-                    start=True,
-                    stop=True,
-                )
+        def product(dst, b, d, codes, sc):
+            nc.tensor.matmul_mx(
+                dst,
+                lhsT=x_codes[b][:, d, :].bitcast(FP8X4),
+                lhsT_scale=x_sc[:, b, d, :],
+                rhs=codes[:].bitcast(FP8X4),
+                rhs_scale=sc[:],
+                start=True,
+                stop=True,
+            )
 
         w1_bf = sb.tile([P, N, PACK], BF16, name="w1_bf", tag="ww", align_bytes=64)
         interleave(nc.scalar.copy, w1_bf, w1_raw, slice(0, SCALAR_SHARE))
@@ -104,13 +103,17 @@ def tile_picked_yoit_grey_p_kernel(tc, x_words, x_scales, w1, w2, depth, offs, o
 
         sig_all = sb.tile([P, BLOCKS, D, N], F32, name="sig_all", tag="sig")
         sig = [sig_all[:, b] for b in range(BLOCKS)]
-        for b in range(BLOCKS):
-            logit = ps.tile([P, D, N], F32, name=f"logit{b}", tag=f"logit{b}")
-            product(logit, b, w2_codes, w2_sc)
-            nc.scalar.activation(sig[b], logit[:], ACT.Sigmoid)
+        for d in range(D):
+            logit = ps.tile([P, N], F32, name=f"logit0{d}", tag=f"early{d}")
+            product(logit[:], 0, d, w2_codes, w2_sc)
+            nc.scalar.activation(sig[0][:, d, :], logit[:], ACT.Sigmoid)
+        logit = ps.tile([P, D, N], F32, name="logit1", tag="early2")
+        for d in range(D):
+            product(logit[:, d, :], 1, d, w2_codes, w2_sc)
+        nc.scalar.activation(sig[1], logit[:], ACT.Sigmoid)
 
         warm2 = sb.tile([P, BLOCKS], F32, name="warm2")
-        nc.scalar.activation(warm2[:], sig_all[:, :, 0, 0], ACT.Abs_reciprocal_sqrt, bias=1.0)
+        nc.scalar.activation(warm2[:], sig_all[:, :, 1, 0], ACT.Abs_reciprocal_sqrt, bias=1.0)
 
         w1_codes = sb.tile([P, N], U32, name="w1_codes", align_bytes=64)
         w1_sc = sb.tile([P, N], U8, name="w1_sc", align_bytes=64)
@@ -119,7 +122,8 @@ def tile_picked_yoit_grey_p_kernel(tc, x_words, x_scales, w1, w2, depth, offs, o
         colour = []
         for b in range(BLOCKS):
             c = ps.tile([P, D, N], F32, name=f"colour{b}")
-            product(c, b, w1_codes, w1_sc)
+            for d in range(D):
+                product(c[:, d, :], b, d, w1_codes, w1_sc)
             colour.append(c)
 
         def turn(dst, parts):
@@ -152,7 +156,7 @@ def tile_picked_yoit_grey_p_kernel(tc, x_words, x_scales, w1, w2, depth, offs, o
         for b in range(BLOCKS):
             tr = sb.tile([P, N], F32, name=f"tr{b}")
             nc.vector.scalar_tensor_tensor(tr[:], sig[b][:, 0, :], 1.0 / OPACITY, shifted[b][:], ALU.subtract, ALU.mult)
-            th = ps.tile([P, MB, P], F32, name=f"through{b}")
+            th = ps.tile([P, MB, P], F32, name=f"through{b}", tag=f"early{3 * b}")
             turn(th, [tr[:]])
             through.append(th)
 
@@ -160,26 +164,27 @@ def tile_picked_yoit_grey_p_kernel(tc, x_words, x_scales, w1, w2, depth, offs, o
         for b in range(BLOCKS):
             cw = sb.tile([P, D, N], F32, name=f"cw{b}")
             nc.vector.scalar_tensor_tensor(cw[:], colour[b][:], GREY, ww[b], ALU.subtract, ALU.mult)
-            nm = ps.tile([P, MB, P], F32, name=f"num{b}", tag=f"logit{b}")
+            nm = ps.tile([P, MB, P], F32, name=f"num{b}", tag=f"early{b + 1}")
             turn(nm, [cw[:, 0, :], cw[:, 1, :]])
             num.append(nm)
 
+        def tiles(name):
+            return [sb.tile([P, MB, P], F32, name=f"{name}{b}") for b in range(BLOCKS)]
+
+        sg, rs, r, g, h, y, res = (tiles(n) for n in ("sg", "rs", "r", "g", "h", "y", "res"))
         for b in range(BLOCKS):
-            sg = sb.tile([P, MB, P], F32, name=f"sg{b}")
-            rs = sb.tile([P, MB, P], F32, name=f"rs{b}")
-            nc.scalar.activation(rs[:], den[b][:], ACT.Abs_reciprocal_sqrt, bias=EPS)
-            nc.scalar.activation(sg[:], den[b][:], ACT.Sign, bias=EPS)
-            r = sb.tile([P, MB, P], F32, name=f"r{b}")
-            nc.scalar.activation(r[:], rs[:], ACT.Square)
-            g = sb.tile([P, MB, P], F32, name=f"g{b}")
-            nc.vector.scalar_tensor_tensor(g[:], through[b][:], 1.0 / OPACITY**2, sg[:], ALU.subtract, ALU.mult)
-            gr = sb.tile([P, MB, P], F32, name=f"gr{b}")
-            nc.vector.scalar_tensor_tensor(gr[:], g[:], -(OPACITY**2), r[:], ALU.mult, ALU.mult)
-            h = sb.tile([P, MB, P], F32, name=f"h{b}")
-            nc.vector.scalar_tensor_tensor(h[:], num[b][:], EPS * GREY, gr[:], ALU.subtract, ALU.mult)
-            res = sb.tile([P, MB, P], F32, name=f"res{b}")
-            if b < BLOCKS - 1:
-                nc.scalar.activation(res[:], h[:], ACT.Copy, bias=GREY)
-            else:
-                nc.vector.tensor_scalar(res[:], h[:], GREY, None, ALU.add)
-            nc.sync.dma_start(out[:, b * P : (b + 1) * P].rearrange("(m p) v -> p m v", p=P), res[:])
+            nc.scalar.activation(sg[b][:], den[b][:], ACT.Sign, bias=EPS)
+        for b in range(BLOCKS):
+            nc.scalar.activation(rs[b][:], den[b][:], ACT.Abs_reciprocal_sqrt, bias=EPS)
+        for b in range(BLOCKS):
+            nc.scalar.activation(r[b][:], rs[b][:], ACT.Square)
+        for b in range(BLOCKS):
+            nc.vector.scalar_tensor_tensor(g[b][:], through[b][:], 1.0 / OPACITY**2, sg[b][:], ALU.subtract, ALU.mult)
+        for b in range(BLOCKS):
+            nc.vector.scalar_tensor_tensor(h[b][:], num[b][:], EPS * GREY, g[b][:], ALU.subtract, ALU.mult)
+        for b in range(BLOCKS):
+            nc.vector.scalar_tensor_tensor(y[b][:], h[b][:], -(OPACITY**2), r[b][:], ALU.mult, ALU.mult)
+        nc.scalar.activation(res[0][:], y[0][:], ACT.Copy, bias=GREY)
+        nc.vector.tensor_scalar(res[1][:], y[1][:], GREY, None, ALU.add)
+        for b, queue in enumerate((nc.scalar, nc.sync)):
+            queue.dma_start(out[:, b * P : (b + 1) * P].rearrange("(m p) v -> p m v", p=P), res[b][:])

@@ -23,7 +23,7 @@ MB = N // P
 OPACITY = 0.95
 EPS = 0.05
 GREY = 0.5
-SCALAR_SHARE = 128
+SCALAR_SHARE = 96
 
 
 def interleave(copy, grouped, raw, cols):
@@ -39,8 +39,8 @@ def tile_picked_yoit_grey_p_kernel(tc, x_words, x_scales, w1, w2, depth, offs, o
         sb = ctx.enter_context(tc.tile_pool(name="sb", bufs=1))
         ps = ctx.enter_context(tc.psum_pool(name="ps", bufs=1))
 
-        scale_table = sb.tile([P, T], U8, name="scale_table", align_bytes=64)
-        nc.gpsimd.memset(scale_table[:].bitcast(I32), 0)
+        scale_table = sb.tile([P, T], U8, name="scale_table", tag="scale_table", align_bytes=64)
+        nc.vector.memset(scale_table[:].bitcast(I32), 0)
         warm_in = sb.tile([P, 1], F32, name="warm_in")
         nc.vector.memset(warm_in[:], 0.0)
 
@@ -68,14 +68,15 @@ def tile_picked_yoit_grey_p_kernel(tc, x_words, x_scales, w1, w2, depth, offs, o
         w2_bf = sb.tile([P, N, PACK], BF16, name="w2_bf", align_bytes=64)
         interleave(nc.scalar.copy, w2_bf, w2_raw, slice(0, N))
 
-        picked_scales = sb.tile([P, S], U8, name="picked_scales", tag="picked_scales", align_bytes=64)
+        picked_scales = sb.tile([P, S], U8, name="picked_scales", align_bytes=64)
         nc.vector.tensor_copy(picked_scales[:], scale_table[:].indirect(offsets[:]))
+
+        w2_codes = sb.tile([P, N], U32, name="w2_codes", tag="scale_table", align_bytes=64)
+        w2_sc = sb.tile([P, N], U8, name="w2_sc", align_bytes=64)
+        nc.vector.quantize_mx(w2_codes[:].bitcast(FP8X4), w2_sc[:], w2_bf[:].rearrange("p n t -> p (n t)"))
+
         x_sc = sb.tile([P, BLOCKS, D, P], U8, name="x_sc", align_bytes=64)
         nc.vector.tensor_copy(x_sc[:], picked_scales[:].rearrange("p (b v d) -> p b d v", b=BLOCKS, d=D))
-
-        w2_codes = sb.tile([P, N], U32, name="w2_codes", align_bytes=64)
-        w2_sc = sb.tile([P, N], U8, name="w2_sc", tag="picked_scales", align_bytes=64)
-        nc.vector.quantize_mx(w2_codes[:].bitcast(FP8X4), w2_sc[:], w2_bf[:].rearrange("p n t -> p (n t)"))
 
         cols = S // 16 // BLOCKS
         x_codes = []
@@ -182,9 +183,11 @@ def tile_picked_yoit_grey_p_kernel(tc, x_words, x_scales, w1, w2, depth, offs, o
             nc.vector.scalar_tensor_tensor(g[b][:], through[b][:], 1.0 / OPACITY**2, sg[b][:], ALU.subtract, ALU.mult)
         for b in range(BLOCKS):
             nc.vector.scalar_tensor_tensor(h[b][:], num[b][:], EPS * GREY, g[b][:], ALU.subtract, ALU.mult)
-        for b in range(BLOCKS):
-            nc.vector.scalar_tensor_tensor(y[b][:], h[b][:], -(OPACITY**2), r[b][:], ALU.mult, ALU.mult)
+        nc.vector.scalar_tensor_tensor(y[0][:], h[0][:], -(OPACITY**2), r[0][:], ALU.mult, ALU.mult)
         nc.scalar.activation(res[0][:], y[0][:], ACT.Copy, bias=GREY)
-        nc.vector.tensor_scalar(res[1][:], y[1][:], GREY, None, ALU.add)
+        for m in range(MB):
+            nc.vector.scalar_tensor_tensor(y[1][:, m], h[1][:, m], -(OPACITY**2), r[1][:, m], ALU.mult, ALU.mult)
+        for m in range(MB):
+            nc.vector.tensor_scalar(res[1][:, m], y[1][:, m], GREY, None, ALU.add)
         for b, queue in enumerate((nc.scalar, nc.sync)):
             queue.dma_start(out[:, b * P : (b + 1) * P].rearrange("(m p) v -> p m v", p=P), res[b][:])

from contextlib import ExitStack

import concourse.mybir as mybir
from concourse.masks import make_identity

K, T, S, D, N = 512, 2048, 512, 2, 256
FLOPS = 2 * 2 * K * N * S

F32 = mybir.dt.float32
BF16 = mybir.dt.bfloat16
I32 = mybir.dt.int32
U32 = mybir.dt.uint32
U16 = mybir.dt.uint16
U8 = mybir.dt.uint8
FP8X4 = mybir.dt.float8_e4m3fn_x4
ALU = mybir.AluOpType
ACT = mybir.ActivationFunctionType

P = 128
PACK = 4
BLOCKS = S // (D * P)
MB = N // P
OPACITY = 0.95
EPS = 0.05
GREY = 0.5
SCALAR_SHARE = 96


def interleave(copy, grouped, raw, cols):
    copy(
        grouped[:, cols, :].rearrange("p (c i) t -> p c t i", i=4),
        raw[:, :, cols].rearrange("p t (c i) -> p c t i", i=4),
    )


def tile_picked_yoit_grey_p_kernel(tc, x_words, x_scales, w1, w2, depth, offs, out):
    nc = tc.nc
    with ExitStack() as ctx:
        sb = ctx.enter_context(tc.tile_pool(name="sb", bufs=1))
        ps = ctx.enter_context(tc.psum_pool(name="ps", bufs=1))

        scale_table = sb.tile([P, T], U8, name="scale_table", tag="scale_table", align_bytes=64)
        nc.vector.memset(scale_table[:].bitcast(I32), 0)
        warm_in = sb.tile([P, 1], F32, name="warm_in")
        nc.vector.memset(warm_in[:], 0.0)

        w2_raw = sb.tile([P, PACK, N], F32, name="w2_raw")
        nc.sync.dma_start(w2_raw[:], w2.rearrange("(p j) n -> p j n", j=PACK))
        offsets = sb.tile([P, S // 16], U16, name="offsets")
        nc.sync.dma_start(offsets[:], offs)
        for q in range(4):
            nc.sync.dma_start(
                scale_table[32 * q : 32 * q + 4, :].bitcast(I32), x_scales[0, 4 * q : 4 * q + 4, :].bitcast(I32)
            )
        word_table = sb.tile([P, T], U32, name="word_table", align_bytes=64)
        nc.sync.dma_start(word_table[:].bitcast(I32), x_words[0].rearrange("p n t -> p (n t)").bitcast(I32))
        w1_raw = sb.tile([P, PACK, N], F32, name="w1_raw", tag="sig")
        nc.sync.dma_start(w1_raw[:], w1.rearrange("(p j) n -> p j n", j=PACK))
        dep = sb.tile([P, BLOCKS, D], F32, name="dep")
        nc.sync.dma_start(dep[:], depth[0].rearrange("(b p d) -> p b d", p=P, d=D))

        warm_out = sb.tile([P, 1], F32, name="warm_out")
        nc.scalar.activation(warm_out[:], warm_in[:], ACT.Sigmoid)

        ident = sb.tile([P, P], F32, name="ident")
        make_identity(nc, ident[:])

        w2_bf = sb.tile([P, N, PACK], BF16, name="w2_bf", align_bytes=64)
        interleave(nc.scalar.copy, w2_bf, w2_raw, slice(0, N))

        picked_scales = sb.tile([P, S], U8, name="picked_scales", align_bytes=64)
        nc.vector.tensor_copy(picked_scales[:], scale_table[:].indirect(offsets[:]))

        w2_codes = sb.tile([P, N], U32, name="w2_codes", tag="scale_table", align_bytes=64)
        w2_sc = sb.tile([P, N], U8, name="w2_sc", align_bytes=64)
        nc.vector.quantize_mx(w2_codes[:].bitcast(FP8X4), w2_sc[:], w2_bf[:].rearrange("p n t -> p (n t)"))

        x_sc = sb.tile([P, BLOCKS, D, P], U8, name="x_sc", align_bytes=64)
        nc.vector.tensor_copy(x_sc[:], picked_scales[:].rearrange("p (b v d) -> p b d v", b=BLOCKS, d=D))

        cols = S // 16 // BLOCKS
        x_codes = []
        for b in range(BLOCKS):
            t = sb.tile([P, D, P], U32, name=f"x_codes{b}", align_bytes=64)
            nc.vector.tensor_copy(
                t[:].rearrange("p d v -> p v d"), word_table[:].indirect(offsets[:, b * cols : (b + 1) * cols])
            )
            x_codes.append(t)

        def product(dst, b, d, codes, sc):
            nc.tensor.matmul_mx(
                dst,
                lhsT=x_codes[b][:, d, :].bitcast(FP8X4),
                lhsT_scale=x_sc[:, b, d, :],
                rhs=codes[:].bitcast(FP8X4),
                rhs_scale=sc[:],
                start=True,
                stop=True,
            )

        w1_bf = sb.tile([P, N, PACK], BF16, name="w1_bf", tag="ww", align_bytes=64)
        interleave(nc.scalar.copy, w1_bf, w1_raw, slice(0, SCALAR_SHARE))
        interleave(nc.vector.tensor_copy, w1_bf, w1_raw, slice(SCALAR_SHARE, N))

        sig_all = sb.tile([P, BLOCKS, D, N], F32, name="sig_all", tag="sig")
        sig = [sig_all[:, b] for b in range(BLOCKS)]
        for d in range(D):
            logit = ps.tile([P, N], F32, name=f"logit0{d}", tag=f"early{d}")
            product(logit[:], 0, d, w2_codes, w2_sc)
            nc.scalar.activation(sig[0][:, d, :], logit[:], ACT.Sigmoid)
        logit = ps.tile([P, D, N], F32, name="logit1", tag="early2")
        for d in range(D):
            product(logit[:, d, :], 1, d, w2_codes, w2_sc)
        nc.scalar.activation(sig[1], logit[:], ACT.Sigmoid)

        warm2 = sb.tile([P, BLOCKS], F32, name="warm2")
        nc.scalar.activation(warm2[:], sig_all[:, :, 1, 0], ACT.Abs_reciprocal_sqrt, bias=1.0)

        w1_codes = sb.tile([P, N], U32, name="w1_codes", align_bytes=64)
        w1_sc = sb.tile([P, N], U8, name="w1_sc", align_bytes=64)
        nc.vector.quantize_mx(w1_codes[:].bitcast(FP8X4), w1_sc[:], w1_bf[:].rearrange("p n t -> p (n t)"))

        colour = []
        for b in range(BLOCKS):
            c = ps.tile([P, D, N], F32, name=f"colour{b}")
            for d in range(D):
                product(c[:, d, :], b, d, w1_codes, w1_sc)
            colour.append(c)

        def turn(dst, parts):
            for m in range(MB):
                for i, part in enumerate(parts):
                    nc.tensor.matmul(
                        dst[:, m, :],
                        lhsT=part[:, m * P : (m + 1) * P],
                        rhs=ident[:],
                        start=(i == 0),
                        stop=(i == len(parts) - 1),
                        is_transpose=True,
                    )

        ww_all = sb.tile([P, BLOCKS, D, N], F32, name="ww_all", tag="ww", align_bytes=64)
        ww, den, shifted = [], [], []
        for b in range(BLOCKS):
            w = ww_all[:, b]
            for d in range(D):
                nc.vector.tensor_scalar(w[:, d, :], sig[b][:, d, :], dep[:, b, d : d + 1], OPACITY, ALU.mult, ALU.mult)
            ww.append(w)
            q = sb.tile([P, N], F32, name=f"q{b}")
            nc.vector.tensor_scalar(q[:], sig[b][:, 1, :], 1.0 / OPACITY, None, ALU.subtract)
            shifted.append(q)
            dn = ps.tile([P, MB, P], F32, name=f"den{b}")
            turn(dn, [w[:, 0, :], w[:, 1, :]])
            den.append(dn)

        through = []
        for b in range(BLOCKS):
            tr = sb.tile([P, N], F32, name=f"tr{b}")
            nc.vector.scalar_tensor_tensor(tr[:], sig[b][:, 0, :], 1.0 / OPACITY, shifted[b][:], ALU.subtract, ALU.mult)
            th = ps.tile([P, MB, P], F32, name=f"through{b}", tag=f"early{3 * b}")
            turn(th, [tr[:]])
            through.append(th)

        num = []
        for b in range(BLOCKS):
            cw = sb.tile([P, D, N], F32, name=f"cw{b}")
            nc.vector.scalar_tensor_tensor(cw[:], colour[b][:], GREY, ww[b], ALU.subtract, ALU.mult)
            nm = ps.tile([P, MB, P], F32, name=f"num{b}", tag=f"early{b + 1}")
            turn(nm, [cw[:, 0, :], cw[:, 1, :]])
            num.append(nm)

        def tiles(name):
            return [sb.tile([P, MB, P], F32, name=f"{name}{b}") for b in range(BLOCKS)]

        sg, rs, r, g, h, y, res = (tiles(n) for n in ("sg", "rs", "r", "g", "h", "y", "res"))
        for b in range(BLOCKS):
            nc.scalar.activation(sg[b][:], den[b][:], ACT.Sign, bias=EPS)
        for b in range(BLOCKS):
            nc.scalar.activation(rs[b][:], den[b][:], ACT.Abs_reciprocal_sqrt, bias=EPS)
        for b in range(BLOCKS):
            nc.scalar.activation(r[b][:], rs[b][:], ACT.Square)
        for b in range(BLOCKS):
            nc.vector.scalar_tensor_tensor(g[b][:], through[b][:], 1.0 / OPACITY**2, sg[b][:], ALU.subtract, ALU.mult)
        for b in range(BLOCKS):
            nc.vector.scalar_tensor_tensor(h[b][:], num[b][:], EPS * GREY, g[b][:], ALU.subtract, ALU.mult)
        nc.vector.scalar_tensor_tensor(y[0][:], h[0][:], -(OPACITY**2), r[0][:], ALU.mult, ALU.mult)
        nc.scalar.activation(res[0][:], y[0][:], ACT.Copy, bias=GREY)
        for m in range(MB):
            nc.vector.scalar_tensor_tensor(y[1][:, m], h[1][:, m], -(OPACITY**2), r[1][:, m], ALU.mult, ALU.mult)
        for m in range(MB):
            nc.vector.tensor_scalar(res[1][:, m], y[1][:, m], GREY, None, ALU.add)
        for b, queue in enumerate((nc.scalar, nc.sync)):
            queue.dma_start(out[:, b * P : (b + 1) * P].rearrange("(m p) v -> p m v", p=P), res[b][:])
